import numpy as np
import ml_dtypes


def mxq(x, axis, fmt="e4m3"):
    dtype, down = {"e4m3": (ml_dtypes.float8_e4m3fn, 7), "e5m2": (ml_dtypes.float8_e5m2, 14)}[fmt]
    v = np.moveaxis(np.asarray(x, np.float32).astype(ml_dtypes.bfloat16).astype(np.float64), axis, -1)
    blocks = v.reshape(v.shape[:-1] + (-1, 32))
    amax = np.abs(blocks).max(-1, keepdims=True)
    byte = np.maximum(np.where(amax > 0, np.frexp(amax)[1] - 1 + 127, 0) - down, 1)
    scale = np.exp2(byte - 127.0)
    codes = (blocks / scale).astype(np.float32).astype(dtype).astype(np.float64)
    return np.moveaxis((codes * scale).reshape(v.shape), -1, axis)


WIDE = False


def mx_kscale(k):
    if not WIDE:
        return np.ones(k)
    levels = np.array([10, -10, 5, -5, 0])
    if k % 512:
        return np.exp2(np.random.permutation(np.resize(levels, k // 32))).repeat(32)
    a = np.empty((k // 512, 16))
    for p in range(k // 512):
        a[p, :8] = np.random.permutation(np.resize(levels, 8))
        for g in range(8):
            far = levels[np.abs(levels - a[p, g]) >= 10]
            a[p, g + 8] = far[np.random.randint(len(far))]
    return np.exp2(a.ravel()).repeat(32)


def f64(x):
    return np.asarray(x).astype(np.float64)


def striped(idx):
    return np.tile(idx.reshape(-1, 16).T, (8, 1)).astype(np.uint16)


def unstriped(offs):
    return offs[:16].T.reshape(-1).astype(np.int64)


def pack_weight(w):
    k, n = w.shape
    w = f64(np.asarray(w, np.float32).astype(ml_dtypes.bfloat16)).reshape(k // 32, 32, n)
    amax = np.abs(w).max(1)
    byte = np.clip(np.where(amax > 0, np.frexp(amax)[1] - 1 + 127 - 7, 1), 1, 254)
    scaled = (w * np.exp2(127.0 - byte)[:, None, :]).reshape(k, n).astype(np.float32)
    words = np.ascontiguousarray(scaled.reshape(k // 512, 128, 4, n).transpose(0, 1, 3, 2)).astype(ml_dtypes.float8_e4m3fn).view(np.uint8)
    return words, np.ascontiguousarray(byte.astype(np.uint8).reshape(k // 512, 16, n))


def unpack_weight(words, scales):
    g, p, n, _ = words.shape
    vals = np.ascontiguousarray(words).view(ml_dtypes.float8_e4m3fn).astype(np.float64) * np.repeat(np.exp2(scales.astype(np.float64) - 127.0), 8, axis=1)[..., None]
    return vals.transpose(0, 1, 3, 2).reshape(g * 512, n)


def planes(y):
    n, m = y.shape
    v = y.astype(np.float32).astype(ml_dtypes.bfloat16).astype(np.float64).reshape(n // 32, 32, m)
    top = np.abs(v).max(1)
    byte = np.clip(np.where(top > 0, np.frexp(top)[1] - 1 + 127 - 7, 1), 1, 254)
    codes = (v * np.exp2(127.0 - byte)[:, None, :]).reshape(n, m).astype(np.float32).astype(ml_dtypes.float8_e4m3fn).view(np.uint8)
    words = codes.reshape(n // 512, 128, 4, m).transpose(0, 1, 3, 2)
    return np.ascontiguousarray(words), np.ascontiguousarray(byte.astype(np.uint8).reshape(n // 512, 16, m))


K, T, S, N, H, W, U = 512, 1024, 512, 512, 512, 1024, 1024


def setup_inputs():
    n = np.random.standard_normal
    s = mx_kscale(K)[:, None]
    u = mx_kscale(H)
    packed_xT = pack_weight(n((K, T)) * s)
    packed_eT = pack_weight(n((K, W)) * s)
    return {
        "x_words": packed_xT[0],
        "x_scales": packed_xT[1],
        "w1": (n((K, N)) / np.sqrt(K) / s).astype(np.float32),
        "e_words": packed_eT[0],
        "e_scales": packed_eT[1],
        "w2": (n((K, N)) / np.sqrt(K) / s).astype(np.float32),
        "unit": (np.random.uniform(0.6, 1.4, (H, 1)) * u[:, None]).astype(np.float32),
        "w3": (n((H, N)) / np.sqrt(H) / u[:, None]).astype(np.float32),
        "offs": striped(np.random.permutation(T)[:S]),
        "nei": striped(np.random.permutation(W)[:S]),
        "c1": striped(np.random.permutation(np.concatenate([np.arange(S), np.random.randint(0, S, U - S)]))),
        "n1": striped(np.random.permutation(np.concatenate([np.arange(S), np.random.randint(0, S, U - S)]))),
        "n2": striped(np.random.permutation(np.concatenate([np.arange(S), np.random.randint(0, S, U - S)]))),
    }


def reference(x_words, x_scales, w1, e_words, e_scales, w2, unit, w3, offs, nei, c1, n1, n2):
    xq = unpack_weight(x_words, x_scales)[:, unstriped(offs)]
    y = mxq(f64(w1), 0, "e4m3").T @ xq
    y_1 = y[:, unstriped(c1)]
    e_nei = unpack_weight(e_words, e_scales)[:, unstriped(nei)]
    ye = mxq(f64(w2), 0, "e4m3").T @ e_nei
    e_1 = ye[:, unstriped(n1)]
    bnd = np.minimum(y_1, e_1)
    e2_ = ye[:, unstriped(n2)]
    hid = f64(unit) * (bnd - (y_1 * e2_))
    out_0 = mxq(f64(w3), 0, "e4m3").T @ mxq(hid, 0, "e4m3")
    return (out_0,) + planes(out_0)

@@ -1,0 +1,251 @@
+from contextlib import ExitStack
+
+import concourse.mybir as mybir
+
+K, T, S, N, U = 512, 1024, 512, 512, 1024
+FLOPS = 2 * K * N * S * 2 + 2 * N * N * U
+
+F32 = mybir.dt.float32
+BF16 = mybir.dt.bfloat16
+I32 = mybir.dt.int32
+U32 = mybir.dt.uint32
+U16 = mybir.dt.uint16
+U8 = mybir.dt.uint8
+FP8X4 = mybir.dt.float8_e4m3fn_x4
+ALU = mybir.AluOpType
+ACT = mybir.ActivationFunctionType
+
+P = 128
+PACK = 4
+SPARE = 16
+SUB = 128
+CHUNKS = [512,256,128,128]
+SCALAR_E1 = [0,0,0,0]
+VECTOR_CAST = [80,80,0]
+
+
+def tile_picked_ymolfrg_min_po_kernel(
+    tc, x_words, x_scales, w1, e_words, e_scales, w2, unit, w3, offs, nei, c1, n1, n2, out_0, out_1, out_2
+):
+    nc = tc.nc
+    with ExitStack() as ctx:
+        keep = ctx.enter_context(tc.tile_pool(name="keep", bufs=1))
+        psum = ctx.enter_context(tc.psum_pool(name="psum", bufs=8))
+
+        def load_list(src, name):
+            tile = keep.tile(list(src.shape), U16, name=name)
+            nc.sync.dma_start(tile[:], src)
+            return tile
+
+        def load_words(src, name):
+            tile = keep.tile([P, T], I32, name=name)
+            nc.sync.dma_start(tile[:], src[0].rearrange("p n t -> p (n t)").bitcast(I32))
+            return tile
+
+        def load_scales(src, name):
+            tile = keep.tile([P, T], U8, name=name)
+            nc.gpsimd.memset(tile[:].bitcast(I32), 0)
+            for q in range(4):
+                nc.gpsimd.dma_start(tile[32 * q : 32 * q + 4, :].bitcast(I32), src[0, 4 * q : 4 * q + 4, :].bitcast(I32))
+            return tile
+
+        def load_weight(src, name):
+            tile = keep.tile([P, PACK, N], F32, name=name)
+            nc.sync.dma_start(tile[:], src.rearrange("(p j) c -> p j c", j=PACK))
+            return tile
+
+        x_scale_table = load_scales(x_scales, "x_scale_table")
+        e_scale_table = load_scales(e_scales, "e_scale_table")
+        offs_sb = load_list(offs, "offs_sb")
+        x_table = load_words(x_words, "x_table")
+        unit_sb = keep.tile([P, PACK], F32, name="unit_sb")
+        nc.sync.dma_start(unit_sb[:], unit.rearrange("(p t) o -> p (t o)", t=PACK))
+        w1_raw = load_weight(w1, "w1_raw")
+        nei_sb = load_list(nei, "nei_sb")
+        e_table = load_words(e_words, "e_table")
+        c1_sb = load_list(c1, "c1_sb")
+        w2_raw = load_weight(w2, "w2_raw")
+        n1_sb = load_list(n1, "n1_sb")
+        n2_sb = load_list(n2, "n2_sb")
+        w3_raw = load_weight(w3, "w3_raw")
+
+        def windows(name):
+            tiles = []
+            for t in range(PACK):
+                tile = keep.tile([P, S + SPARE], F32, name=f"{name}{t}")
+                nc.gpsimd.memset(tile[:, S:], 0.0)
+                tiles.append(tile)
+            return tiles
+
+        neg_y = windows("neg_y")
+        ye = windows("ye")
+        gain = windows("gain")
+
+        neg_unit = keep.tile([P, PACK], F32, name="neg_unit")
+        nc.scalar.activation(neg_unit[:], unit_sb[:], ACT.Copy, scale=-1.0)
+
+        def pick(table, scale_table, offsets, name):
+            words = keep.tile([P, S], U32, name=name + "_words", align_bytes=64)
+            scales = keep.tile([P, S], U8, name=name + "_scales", align_bytes=64)
+            nc.vector.tensor_copy(words[:], table[:].bitcast(U32).indirect(offsets[:]))
+            nc.vector.tensor_copy(scales[:], scale_table[:].indirect(offsets[:]))
+            return words, scales
+
+        def round_weight(raw, on_vector, name):
+            dealt = keep.tile([P, PACK * P * PACK], BF16, name=name + "_dealt", align_bytes=64)
+            src = raw[:].rearrange("p j (m t) -> p m j t", t=PACK)
+            dst = dealt[:].rearrange("p (t m j) -> p m j t", t=PACK, j=PACK)
+            if on_vector > 0:
+                nc.vector.tensor_copy(dst[:, :on_vector], src[:, :on_vector])
+            if on_vector < P:
+                nc.scalar.copy(dst[:, on_vector:], src[:, on_vector:])
+            return dealt
+
+        def quantise_weight(dealt, name):
+            words = keep.tile([P, N], U32, name=name + "_words", align_bytes=64)
+            scales = keep.tile([P, N], U8, name=name + "_scales", align_bytes=64)
+            for h in range(2):
+                cols = slice(h * N // 2, (h + 1) * N // 2)
+                nc.vector.quantize_mx(words[:, cols].bitcast(FP8X4), scales[:, cols], dealt[:, PACK * cols.start : PACK * cols.stop])
+            return words, scales
+
+        def product(acc, weight, t, moving, cols):
+            rows = slice(t * P, (t + 1) * P)
+            nc.tensor.matmul_mx(
+                out=acc,
+                lhsT=weight[0][:, rows].bitcast(FP8X4),
+                lhsT_scale=weight[1][:, rows],
+                rhs=moving[0][:, cols].bitcast(FP8X4),
+                rhs_scale=moving[1][:, cols],
+                start=True,
+                stop=True,
+            )
+
+        x_picked = pick(x_table, x_scale_table, offs_sb, "x_picked")
+        w1_q = quantise_weight(round_weight(w1_raw, VECTOR_CAST[0], "w1"), "w1")
+        for t in range(PACK):
+            bank = psum.tile([P, S], F32, name="bank")
+            product(bank[:], w1_q, t, x_picked, slice(0, S))
+            nc.scalar.activation(neg_y[t][:, :S], bank[:], ACT.Copy, scale=-1.0)
+
+        e_picked = pick(e_table, e_scale_table, nei_sb, "e_picked")
+        w2_q = quantise_weight(round_weight(w2_raw, VECTOR_CAST[1], "w2"), "w2")
+
+        starts = [sum(CHUNKS[:c]) for c in range(len(CHUNKS))]
+
+        def entries(offsets, c):
+            return offsets[:, starts[c] // 16 : (starts[c] + CHUNKS[c]) // 16]
+
+        core = [keep.tile([P, PACK, n], F32, name=f"core{c}") for c, n in enumerate(CHUNKS)]
+        first = [keep.tile([P, PACK, n], F32, name=f"first{c}") if SCALAR_E1[c] else None for c, n in enumerate(CHUNKS)]
+
+        def fetch_core(c, t):
+            nc.scalar.activation(core[c][:, t, :], neg_y[t][:].indirect(entries(c1_sb, c)), ACT.Copy)
+
+        def fetch_first(c, t):
+            if t < SCALAR_E1[c]:
+                nc.scalar.activation(first[c][:, t, :], ye[t][:].indirect(entries(n1_sb, c)), ACT.Copy)
+
+        fetch_core(0, 0)
+        for t in range(PACK):
+            bank = psum.tile([P, S], F32, name="bank")
+            product(bank[:], w2_q, t, e_picked, slice(0, S))
+            nc.vector.tensor_copy(ye[t][:, :S], bank[:])
+            nc.scalar.activation(gain[t][:, :S], bank[:], ACT.Identity, scale=unit_sb[:, t : t + 1], bias=neg_unit[:, t : t + 1])
+            if t + 1 < PACK:
+                fetch_core(0, t + 1)
+        for t in range(PACK):
+            fetch_first(0, t)
+        w3_dealt = round_weight(w3_raw, VECTOR_CAST[2], "w3")
+
+        out_words = keep.tile([P, U], U32, name="out_words", align_bytes=64)
+        out_scales = keep.tile([P, U], U8, name="out_scales", align_bytes=64)
+        out_rows = out_0.rearrange("(p t) c -> p t c", t=PACK)
+        word_rows = out_1[0].rearrange("p n t -> p (n t)").bitcast(I32)
+        state = {}
+
+        def hidden_steps(c):
+            n = CHUNKS[c]
+            gap = keep.tile([P, PACK, n], F32, name=f"gap{c}")
+            low = keep.tile([P, PACK, n], F32, name=f"low{c}")
+            kept = keep.tile([P, PACK, n], F32, name=f"kept{c}")
+            hid = keep.tile([P, PACK * n], BF16, name=f"hid{c}", align_bytes=64)
+            words = keep.tile([P, n], U32, name=f"hid_words{c}", align_bytes=64)
+            scales = keep.tile([P, n], U8, name=f"hid_scales{c}", align_bytes=64)
+            state[c] = (words, scales)
+
+            def gap_of(t):
+                if t < SCALAR_E1[c]:
+                    nc.vector.tensor_tensor(gap[:, t, :], first[c][:, t, :], core[c][:, t, :], ALU.add)
+                else:
+                    nc.vector.tensor_tensor(gap[:, t, :], ye[t][:].indirect(entries(n1_sb, c)), core[c][:, t, :], ALU.add)
+
+            def rest_of(t):
+                nc.vector.tensor_tensor(kept[:, t, :], gain[t][:].indirect(entries(n2_sb, c)), core[c][:, t, :], ALU.mult)
+                nc.vector.tensor_scalar(low[:, t, :], gap[:, t, :], 0.0, unit_sb[:, t : t + 1], ALU.min, ALU.mult)
+
+            def weave():
+                walk = "p t (c i) -> p c t i"
+                nc.vector.tensor_tensor(
+                    hid[:].rearrange("p (c i t) -> p c t i", i=2, t=PACK),
+                    kept[:].rearrange(walk, i=2),
+                    low[:].rearrange(walk, i=2),
+                    ALU.add,
+                )
+
+            def quantise():
+                nc.vector.quantize_mx(words[:].bitcast(FP8X4), scales[:], hid[:])
+
+            return gap_of, rest_of, weave, quantise
+
+        def last_product(c, w3_q):
+            n = CHUNKS[c]
+            result = keep.tile([P, PACK, n], F32, name=f"result{c}")
+            rounded = keep.tile([P, PACK * n], BF16, name=f"rounded{c}", align_bytes=64)
+            for s0 in range(0, n, SUB):
+                bank = psum.tile([P, PACK, SUB], F32, name="bank")
+                for t in range(PACK):
+                    product(bank[:, t, :], w3_q, t, state[c], slice(s0, s0 + SUB))
+                nc.scalar.copy(
+                    rounded[:, PACK * s0 : PACK * (s0 + SUB)].rearrange("p (c t) -> p c t", t=PACK),
+                    bank[:].rearrange("p t c -> p c t"),
+                )
+                nc.scalar.copy(result[:, :, s0 : s0 + SUB], bank[:])
+            cols = slice(starts[c], starts[c] + n)
+            nc.sync.dma_start(out_rows[:, :, cols], result[:])
+
+            def planes():
+                nc.vector.quantize_mx(out_words[:, cols].bitcast(FP8X4), out_scales[:, cols], rounded[:])
+                nc.sync.dma_start(word_rows[:, cols], out_words[:, cols].bitcast(I32))
+
+            return planes
+
+        steps = hidden_steps(0)
+        steps[0](0)
+        pending = None
+        w3_q = None
+        for c in range(len(CHUNKS)):
+            gap_of, rest_of, weave, quantise = steps
+            more = c + 1 < len(CHUNKS)
+            if more:
+                for t in range(PACK):
+                    fetch_core(c + 1, t)
+                    fetch_first(c + 1, t)
+            for t in range(PACK):
+                rest_of(t)
+                if t + 1 < PACK:
+                    gap_of(t + 1)
+            if pending is not None:
+                pending()
+            if w3_q is None:
+                w3_q = quantise_weight(w3_dealt, "w3")
+            weave()
+            if more:
+                steps = hidden_steps(c + 1)
+                steps[0](0)
+            quantise()
+            pending = last_product(c, w3_q)
+        pending()
+        for q in range(4):
+            queue = nc.sync if q % 2 == 0 else nc.scalar
+            queue.dma_start(out_2[0, 4 * q : 4 * q + 4, :].bitcast(I32), out_scales[32 * q : 32 * q + 4, :].bitcast(I32))

@@ -19,9 +19,10 @@ P = 128
 PACK = 4
 SPARE = 16
 SUB = 128
-CHUNKS = [512,256,128,128]
-SCALAR_E1 = [0,0,0,0]
-VECTOR_CAST = [80,80,0]
+CHUNKS = [512,384,128]
+SCALAR_E1 = [0,3,4]
+VECTOR_YE = 1
+VECTOR_CAST = [88,96,0]
 
 
 def tile_picked_ymolfrg_min_po_kernel(
@@ -42,11 +43,11 @@ def tile_picked_ymolfrg_min_po_kernel(
             nc.sync.dma_start(tile[:], src[0].rearrange("p n t -> p (n t)").bitcast(I32))
             return tile
 
-        def load_scales(src, name):
+        def load_scales(src, name, queue):
             tile = keep.tile([P, T], U8, name=name)
-            nc.gpsimd.memset(tile[:].bitcast(I32), 0)
+            nc.vector.memset(tile[:].bitcast(I32), 0)
             for q in range(4):
-                nc.gpsimd.dma_start(tile[32 * q : 32 * q + 4, :].bitcast(I32), src[0, 4 * q : 4 * q + 4, :].bitcast(I32))
+                queue.dma_start(tile[32 * q : 32 * q + 4, :].bitcast(I32), src[0, 4 * q : 4 * q + 4, :].bitcast(I32))
             return tile
 
         def load_weight(src, name):
@@ -54,17 +55,17 @@ def tile_picked_ymolfrg_min_po_kernel(
             nc.sync.dma_start(tile[:], src.rearrange("(p j) c -> p j c", j=PACK))
             return tile
 
-        x_scale_table = load_scales(x_scales, "x_scale_table")
-        e_scale_table = load_scales(e_scales, "e_scale_table")
         offs_sb = load_list(offs, "offs_sb")
+        x_scale_table = load_scales(x_scales, "x_scale_table", nc.sync)
         x_table = load_words(x_words, "x_table")
+        w1_raw = load_weight(w1, "w1_raw")
+        e_table = load_words(e_words, "e_table")
+        nei_sb = load_list(nei, "nei_sb")
+        e_scale_table = load_scales(e_scales, "e_scale_table", nc.sync)
+        w2_raw = load_weight(w2, "w2_raw")
+        c1_sb = load_list(c1, "c1_sb")
         unit_sb = keep.tile([P, PACK], F32, name="unit_sb")
         nc.sync.dma_start(unit_sb[:], unit.rearrange("(p t) o -> p (t o)", t=PACK))
-        w1_raw = load_weight(w1, "w1_raw")
-        nei_sb = load_list(nei, "nei_sb")
-        e_table = load_words(e_words, "e_table")
-        c1_sb = load_list(c1, "c1_sb")
-        w2_raw = load_weight(w2, "w2_raw")
         n1_sb = load_list(n1, "n1_sb")
         n2_sb = load_list(n2, "n2_sb")
         w3_raw = load_weight(w3, "w3_raw")
@@ -73,7 +74,7 @@ def tile_picked_ymolfrg_min_po_kernel(
             tiles = []
             for t in range(PACK):
                 tile = keep.tile([P, S + SPARE], F32, name=f"{name}{t}")
-                nc.gpsimd.memset(tile[:, S:], 0.0)
+                nc.vector.memset(tile[:, S:], 0.0)
                 tiles.append(tile)
             return tiles
 
@@ -84,15 +85,15 @@ def tile_picked_ymolfrg_min_po_kernel(
         neg_unit = keep.tile([P, PACK], F32, name="neg_unit")
         nc.scalar.activation(neg_unit[:], unit_sb[:], ACT.Copy, scale=-1.0)
 
-        def pick(table, scale_table, offsets, name):
-            words = keep.tile([P, S], U32, name=name + "_words", align_bytes=64)
+        def pick(table, scale_table, offsets, name, tag):
+            words = keep.tile([P, S], U32, name=name + "_words", tag=tag, align_bytes=64)
             scales = keep.tile([P, S], U8, name=name + "_scales", align_bytes=64)
             nc.vector.tensor_copy(words[:], table[:].bitcast(U32).indirect(offsets[:]))
             nc.vector.tensor_copy(scales[:], scale_table[:].indirect(offsets[:]))
             return words, scales
 
         def round_weight(raw, on_vector, name):
-            dealt = keep.tile([P, PACK * P * PACK], BF16, name=name + "_dealt", align_bytes=64)
+            dealt = keep.tile([P, PACK * P * PACK], BF16, name=name + "_dealt", tag=name + "_dealt", align_bytes=64)
             src = raw[:].rearrange("p j (m t) -> p m j t", t=PACK)
             dst = dealt[:].rearrange("p (t m j) -> p m j t", t=PACK, j=PACK)
             if on_vector > 0:
@@ -101,11 +102,11 @@ def tile_picked_ymolfrg_min_po_kernel(
                 nc.scalar.copy(dst[:, on_vector:], src[:, on_vector:])
             return dealt
 
-        def quantise_weight(dealt, name):
+        def quantise_weight(dealt, name, parts):
             words = keep.tile([P, N], U32, name=name + "_words", align_bytes=64)
             scales = keep.tile([P, N], U8, name=name + "_scales", align_bytes=64)
-            for h in range(2):
-                cols = slice(h * N // 2, (h + 1) * N // 2)
+            for h in range(parts):
+                cols = slice(h * N // parts, (h + 1) * N // parts)
                 nc.vector.quantize_mx(words[:, cols].bitcast(FP8X4), scales[:, cols], dealt[:, PACK * cols.start : PACK * cols.stop])
             return words, scales
 
@@ -121,15 +122,15 @@ def tile_picked_ymolfrg_min_po_kernel(
                 stop=True,
             )
 
-        x_picked = pick(x_table, x_scale_table, offs_sb, "x_picked")
-        w1_q = quantise_weight(round_weight(w1_raw, VECTOR_CAST[0], "w1"), "w1")
+        x_picked = pick(x_table, x_scale_table, offs_sb, "x_picked", "x_picked_words")
+        w1_q = quantise_weight(round_weight(w1_raw, VECTOR_CAST[0], "w1"), "w1", 2)
         for t in range(PACK):
             bank = psum.tile([P, S], F32, name="bank")
             product(bank[:], w1_q, t, x_picked, slice(0, S))
             nc.scalar.activation(neg_y[t][:, :S], bank[:], ACT.Copy, scale=-1.0)
 
-        e_picked = pick(e_table, e_scale_table, nei_sb, "e_picked")
-        w2_q = quantise_weight(round_weight(w2_raw, VECTOR_CAST[1], "w2"), "w2")
+        e_picked = pick(e_table, e_scale_table, nei_sb, "e_picked", "w1_dealt")
+        w2_q = quantise_weight(round_weight(w2_raw, VECTOR_CAST[1], "w2"), "w2", 2)
 
         starts = [sum(CHUNKS[:c]) for c in range(len(CHUNKS))]
 
@@ -150,7 +151,7 @@ def tile_picked_ymolfrg_min_po_kernel(
         for t in range(PACK):
             bank = psum.tile([P, S], F32, name="bank")
             product(bank[:], w2_q, t, e_picked, slice(0, S))
-            nc.vector.tensor_copy(ye[t][:, :S], bank[:])
+            (nc.vector.tensor_copy if t < VECTOR_YE else nc.scalar.copy)(ye[t][:, :S], bank[:])
             nc.scalar.activation(gain[t][:, :S], bank[:], ACT.Identity, scale=unit_sb[:, t : t + 1], bias=neg_unit[:, t : t + 1])
             if t + 1 < PACK:
                 fetch_core(0, t + 1)
@@ -206,7 +207,8 @@ def tile_picked_ymolfrg_min_po_kernel(
                 bank = psum.tile([P, PACK, SUB], F32, name="bank")
                 for t in range(PACK):
                     product(bank[:, t, :], w3_q, t, state[c], slice(s0, s0 + SUB))
-                nc.scalar.copy(
+                rounder = nc.vector.tensor_copy if c + 1 == len(CHUNKS) else nc.scalar.copy
+                rounder(
                     rounded[:, PACK * s0 : PACK * (s0 + SUB)].rearrange("p (c t) -> p c t", t=PACK),
                     bank[:].rearrange("p t c -> p c t"),
                 )
@@ -235,16 +237,16 @@ def tile_picked_ymolfrg_min_po_kernel(
                 rest_of(t)
                 if t + 1 < PACK:
                     gap_of(t + 1)
-            if pending is not None:
-                pending()
             if w3_q is None:
-                w3_q = quantise_weight(w3_dealt, "w3")
+                w3_q = quantise_weight(w3_dealt, "w3", 1)
             weave()
             if more:
                 steps = hidden_steps(c + 1)
                 steps[0](0)
             quantise()
-            pending = last_product(c, w3_q)
+            earlier, pending = pending, last_product(c, w3_q)
+            if earlier is not None:
+                earlier()
         pending()
         for q in range(4):
             queue = nc.sync if q % 2 == 0 else nc.scalar

@@ -19,9 +19,12 @@ P = 128
 PACK = 4
 SPARE = 16
 SUB = 128
-CHUNKS = [512,384,128]
-SCALAR_E1 = [0,3,4]
+CHUNKS = [512,256,256]
+PIECES = [[512],[256],[128,128]]
+GAP_TILES = [1,1,2]
+SCALAR_E1 = [0,4,4]
 VECTOR_YE = 1
+ROUNDER = ["scalar","scalar","sbuf","split"]
 VECTOR_CAST = [88,96,0]
 
 
@@ -144,7 +147,7 @@ def tile_picked_ymolfrg_min_po_kernel(
             nc.scalar.activation(core[c][:, t, :], neg_y[t][:].indirect(entries(c1_sb, c)), ACT.Copy)
 
         def fetch_first(c, t):
-            if t < SCALAR_E1[c]:
+            if t >= PACK - SCALAR_E1[c]:
                 nc.scalar.activation(first[c][:, t, :], ye[t][:].indirect(entries(n1_sb, c)), ACT.Copy)
 
         fetch_core(0, 0)
@@ -163,71 +166,84 @@ def tile_picked_ymolfrg_min_po_kernel(
         out_scales = keep.tile([P, U], U8, name="out_scales", align_bytes=64)
         out_rows = out_0.rearrange("(p t) c -> p t c", t=PACK)
         word_rows = out_1[0].rearrange("p n t -> p (n t)").bitcast(I32)
-        state = {}
 
-        def hidden_steps(c):
+        def chunk_steps(c):
             n = CHUNKS[c]
             gap = keep.tile([P, PACK, n], F32, name=f"gap{c}")
             low = keep.tile([P, PACK, n], F32, name=f"low{c}")
             kept = keep.tile([P, PACK, n], F32, name=f"kept{c}")
-            hid = keep.tile([P, PACK * n], BF16, name=f"hid{c}", align_bytes=64)
-            words = keep.tile([P, n], U32, name=f"hid_words{c}", align_bytes=64)
-            scales = keep.tile([P, n], U8, name=f"hid_scales{c}", align_bytes=64)
-            state[c] = (words, scales)
 
             def gap_of(t):
-                if t < SCALAR_E1[c]:
-                    nc.vector.tensor_tensor(gap[:, t, :], first[c][:, t, :], core[c][:, t, :], ALU.add)
-                else:
+                if t < PACK - SCALAR_E1[c]:
                     nc.vector.tensor_tensor(gap[:, t, :], ye[t][:].indirect(entries(n1_sb, c)), core[c][:, t, :], ALU.add)
+                elif t % GAP_TILES[c] == 0:
+                    tiles = slice(t, t + GAP_TILES[c])
+                    nc.vector.tensor_tensor(gap[:, tiles, :], first[c][:, tiles, :], core[c][:, tiles, :], ALU.add)
 
             def rest_of(t):
                 nc.vector.tensor_tensor(kept[:, t, :], gain[t][:].indirect(entries(n2_sb, c)), core[c][:, t, :], ALU.mult)
                 nc.vector.tensor_scalar(low[:, t, :], gap[:, t, :], 0.0, unit_sb[:, t : t + 1], ALU.min, ALU.mult)
 
+            return gap_of, rest_of, low, kept
+
+        def piece_steps(c, low, kept, p0, n, rounder):
+            name = f"{c}_{p0}"
+            hid = keep.tile([P, PACK * n], BF16, name="hid" + name, align_bytes=64)
+            words = keep.tile([P, n], U32, name="hid_words" + name, align_bytes=64)
+            scales = keep.tile([P, n], U8, name="hid_scales" + name, align_bytes=64)
+            result = keep.tile([P, PACK, n], F32, name="result" + name)
+            rounded = keep.tile([P, PACK * n], BF16, name="rounded" + name, align_bytes=64)
+            cols = slice(starts[c] + p0, starts[c] + p0 + n)
+
             def weave():
                 walk = "p t (c i) -> p c t i"
                 nc.vector.tensor_tensor(
                     hid[:].rearrange("p (c i t) -> p c t i", i=2, t=PACK),
-                    kept[:].rearrange(walk, i=2),
-                    low[:].rearrange(walk, i=2),
+                    kept[:, :, p0 : p0 + n].rearrange(walk, i=2),
+                    low[:, :, p0 : p0 + n].rearrange(walk, i=2),
                     ALU.add,
                 )
 
-            def quantise():
+            def multiply(w3_q):
                 nc.vector.quantize_mx(words[:].bitcast(FP8X4), scales[:], hid[:])
-
-            return gap_of, rest_of, weave, quantise
-
-        def last_product(c, w3_q):
-            n = CHUNKS[c]
-            result = keep.tile([P, PACK, n], F32, name=f"result{c}")
-            rounded = keep.tile([P, PACK * n], BF16, name=f"rounded{c}", align_bytes=64)
-            for s0 in range(0, n, SUB):
-                bank = psum.tile([P, PACK, SUB], F32, name="bank")
-                for t in range(PACK):
-                    product(bank[:, t, :], w3_q, t, state[c], slice(s0, s0 + SUB))
-                rounder = nc.vector.tensor_copy if c + 1 == len(CHUNKS) else nc.scalar.copy
-                rounder(
-                    rounded[:, PACK * s0 : PACK * (s0 + SUB)].rearrange("p (c t) -> p c t", t=PACK),
-                    bank[:].rearrange("p t c -> p c t"),
-                )
-                nc.scalar.copy(result[:, :, s0 : s0 + SUB], bank[:])
-            cols = slice(starts[c], starts[c] + n)
-            nc.sync.dma_start(out_rows[:, :, cols], result[:])
+                for s0 in range(0, n, SUB):
+                    sub = slice(s0, s0 + SUB)
+                    if rounder == "split":
+                        for half, copy in ((0, nc.scalar.copy), (1, nc.vector.tensor_copy)):
+                            bank = psum.tile([P, 2, SUB], F32, name="bank")
+                            for t in range(2):
+                                product(bank[:, t, :], w3_q, 2 * half + t, (words, scales), sub)
+                            copy(result[:, 2 * half : 2 * half + 2, sub], bank[:])
+                        continue
+                    bank = psum.tile([P, PACK, SUB], F32, name="bank")
+                    for t in range(PACK):
+                        product(bank[:, t, :], w3_q, t, (words, scales), sub)
+                    if rounder == "scalar":
+                        nc.scalar.copy(
+                            rounded[:, PACK * s0 : PACK * (s0 + SUB)].rearrange("p (c t) -> p c t", t=PACK),
+                            bank[:].rearrange("p t c -> p c t"),
+                        )
+                    nc.scalar.copy(result[:, :, sub], bank[:])
+                nc.sync.dma_start(out_rows[:, :, cols], result[:])
 
             def planes():
+                if rounder != "scalar":
+                    nc.vector.tensor_copy(
+                        rounded[:].rearrange("p (c i t) -> p c t i", i=2, t=PACK),
+                        result[:].rearrange("p t (c i) -> p c t i", i=2),
+                    )
                 nc.vector.quantize_mx(out_words[:, cols].bitcast(FP8X4), out_scales[:, cols], rounded[:])
                 nc.sync.dma_start(word_rows[:, cols], out_words[:, cols].bitcast(I32))
 
-            return planes
+            return weave, multiply, planes
 
-        steps = hidden_steps(0)
+        steps = chunk_steps(0)
         steps[0](0)
         pending = None
         w3_q = None
+        piece = 0
         for c in range(len(CHUNKS)):
-            gap_of, rest_of, weave, quantise = steps
+            gap_of, rest_of, low, kept = steps
             more = c + 1 < len(CHUNKS)
             if more:
                 for t in range(PACK):
@@ -239,14 +255,23 @@ def tile_picked_ymolfrg_min_po_kernel(
                     gap_of(t + 1)
             if w3_q is None:
                 w3_q = quantise_weight(w3_dealt, "w3", 1)
-            weave()
-            if more:
-                steps = hidden_steps(c + 1)
-                steps[0](0)
-            quantise()
-            earlier, pending = pending, last_product(c, w3_q)
-            if earlier is not None:
-                earlier()
+            p0 = 0
+            made = []
+            for n in PIECES[c]:
+                made.append(piece_steps(c, low, kept, p0, n, ROUNDER[piece]))
+                p0 = p0 + n
+                piece = piece + 1
+            made[0][0]()
+            for i, (weave, multiply, planes) in enumerate(made):
+                if i + 1 < len(made):
+                    made[i + 1][0]()
+                elif more:
+                    steps = chunk_steps(c + 1)
+                    steps[0](0)
+                multiply(w3_q)
+                if pending is not None:
+                    pending()
+                pending = planes
         pending()
         for q in range(4):
             queue = nc.sync if q % 2 == 0 else nc.scalar

@@ -59,8 +59,8 @@ def tile_picked_ymolfrg_min_po_kernel(
             return tile
 
         offs_sb = load_list(offs, "offs_sb")
-        x_scale_table = load_scales(x_scales, "x_scale_table", nc.sync)
         x_table = load_words(x_words, "x_table")
+        x_scale_table = load_scales(x_scales, "x_scale_table", nc.sync)
         w1_raw = load_weight(w1, "w1_raw")
         e_table = load_words(e_words, "e_table")
         nei_sb = load_list(nei, "nei_sb")
@@ -97,12 +97,12 @@ def tile_picked_ymolfrg_min_po_kernel(
 
         def round_weight(raw, on_vector, name):
             dealt = keep.tile([P, PACK * P * PACK], BF16, name=name + "_dealt", tag=name + "_dealt", align_bytes=64)
-            src = raw[:].rearrange("p j (m t) -> p m j t", t=PACK)
-            dst = dealt[:].rearrange("p (t m j) -> p m j t", t=PACK, j=PACK)
+            src = raw[:].rearrange("p j (m h i) -> p h m j i", h=2, i=2)
+            dst = dealt[:].rearrange("p (h i m j) -> p h m j i", h=2, i=2, j=PACK)
             if on_vector > 0:
-                nc.vector.tensor_copy(dst[:, :on_vector], src[:, :on_vector])
+                nc.vector.tensor_copy(dst[:, :, :on_vector], src[:, :, :on_vector])
             if on_vector < P:
-                nc.scalar.copy(dst[:, on_vector:], src[:, on_vector:])
+                nc.scalar.copy(dst[:, :, on_vector:], src[:, :, on_vector:])
             return dealt
 
         def quantise_weight(dealt, name, parts):
@@ -220,8 +220,8 @@ def tile_picked_ymolfrg_min_po_kernel(
                         product(bank[:, t, :], w3_q, t, (words, scales), sub)
                     if rounder == "scalar":
                         nc.scalar.copy(
-                            rounded[:, PACK * s0 : PACK * (s0 + SUB)].rearrange("p (c t) -> p c t", t=PACK),
-                            bank[:].rearrange("p t c -> p c t"),
+                            rounded[:, PACK * s0 : PACK * (s0 + SUB)].rearrange("p (c i t) -> p c t i", i=2, t=PACK),
+                            bank[:].rearrange("p t (c i) -> p c t i", i=2),
                         )
                     nc.scalar.copy(result[:, :, sub], bank[:])
                 nc.sync.dma_start(out_rows[:, :, cols], result[:])

@@ -3,7 +3,7 @@ from contextlib import ExitStack
 import concourse.mybir as mybir
 
 K, T, S, N, U = 512, 1024, 512, 512, 1024
-FLOPS = 2 * K * N * S * 2 + 2 * N * N * U
+FLOPS = 2 * (2 * K * N * S) + 2 * N * N * U
 
 F32 = mybir.dt.float32
 BF16 = mybir.dt.bfloat16
@@ -17,15 +17,23 @@ ACT = mybir.ActivationFunctionType
 
 P = 128
 PACK = 4
+QUADRANT = 32
+LIST_ROWS = 16
+BANKS = 8
 SPARE = 16
-SUB = 128
-CHUNKS = [512,256,256]
-PIECES = [[512],[256],[128,128]]
-GAP_TILES = [1,1,2]
-SCALAR_E1 = [0,4,4]
-VECTOR_YE = 1
-ROUNDER = ["scalar","scalar","sbuf","split"]
-VECTOR_CAST = [88,96,0]
+BANK_COLS = 128
+CHUNKS = (512, 256, 256)
+VECTOR_GROUPS_W1, VECTOR_GROUPS_W2, VECTOR_GROUPS_W3 = 52, 96, 0
+WOVEN = "p (c i t) -> p c t i"
+ROW_TILES = "p t (c i) -> p c t i"
+
+
+def woven(ap):
+    return ap.rearrange(WOVEN, i=2, t=PACK)
+
+
+def row_tiles(ap):
+    return ap.rearrange(ROW_TILES, i=2)
 
 
 def tile_picked_ymolfrg_min_po_kernel(
@@ -34,7 +42,7 @@ def tile_picked_ymolfrg_min_po_kernel(
     nc = tc.nc
     with ExitStack() as ctx:
         keep = ctx.enter_context(tc.tile_pool(name="keep", bufs=1))
-        psum = ctx.enter_context(tc.psum_pool(name="psum", bufs=8))
+        psum = ctx.enter_context(tc.psum_pool(name="psum", bufs=BANKS))
 
         def load_list(src, name):
             tile = keep.tile(list(src.shape), U16, name=name)
@@ -46,32 +54,37 @@ def tile_picked_ymolfrg_min_po_kernel(
             nc.sync.dma_start(tile[:], src[0].rearrange("p n t -> p (n t)").bitcast(I32))
             return tile
 
-        def load_scales(src, name, queue):
+        def load_scales(src, name):
             tile = keep.tile([P, T], U8, name=name)
             nc.vector.memset(tile[:].bitcast(I32), 0)
-            for q in range(4):
-                queue.dma_start(tile[32 * q : 32 * q + 4, :].bitcast(I32), src[0, 4 * q : 4 * q + 4, :].bitcast(I32))
+            for q in range(P // QUADRANT):
+                rows = tile[QUADRANT * q : QUADRANT * q + PACK, :]
+                nc.sync.dma_start(rows.bitcast(I32), src[0, PACK * q : PACK * (q + 1), :].bitcast(I32))
             return tile
 
-        def load_weight(src, name):
-            tile = keep.tile([P, PACK, N], F32, name=name)
-            nc.sync.dma_start(tile[:], src.rearrange("(p j) c -> p j c", j=PACK))
-            return tile
+        def load_weight(src, name, parts):
+            tiles = []
+            for part in range(parts):
+                tile = keep.tile([P, PACK, N // parts], F32, name=f"{name}{part}")
+                cols = slice(part * N // parts, (part + 1) * N // parts)
+                nc.sync.dma_start(tile[:], src.rearrange("(p j) c -> p j c", j=PACK)[:, :, cols])
+                tiles.append(tile)
+            return tiles
 
         offs_sb = load_list(offs, "offs_sb")
         x_table = load_words(x_words, "x_table")
-        x_scale_table = load_scales(x_scales, "x_scale_table", nc.sync)
-        w1_raw = load_weight(w1, "w1_raw")
+        x_scale_table = load_scales(x_scales, "x_scale_table")
+        w1_raw = load_weight(w1, "w1_raw", 2)
         e_table = load_words(e_words, "e_table")
         nei_sb = load_list(nei, "nei_sb")
-        e_scale_table = load_scales(e_scales, "e_scale_table", nc.sync)
-        w2_raw = load_weight(w2, "w2_raw")
+        e_scale_table = load_scales(e_scales, "e_scale_table")
+        w2_raw = load_weight(w2, "w2_raw", 1)
         c1_sb = load_list(c1, "c1_sb")
         unit_sb = keep.tile([P, PACK], F32, name="unit_sb")
         nc.sync.dma_start(unit_sb[:], unit.rearrange("(p t) o -> p (t o)", t=PACK))
         n1_sb = load_list(n1, "n1_sb")
         n2_sb = load_list(n2, "n2_sb")
-        w3_raw = load_weight(w3, "w3_raw")
+        w3_raw = load_weight(w3, "w3_raw", 1)
 
         def windows(name):
             tiles = []
@@ -95,22 +108,26 @@ def tile_picked_ymolfrg_min_po_kernel(
             nc.vector.tensor_copy(scales[:], scale_table[:].indirect(offsets[:]))
             return words, scales
 
-        def round_weight(raw, on_vector, name):
-            dealt = keep.tile([P, PACK * P * PACK], BF16, name=name + "_dealt", tag=name + "_dealt", align_bytes=64)
-            src = raw[:].rearrange("p j (m h i) -> p h m j i", h=2, i=2)
+        def round_weight(raw, vector_groups, name):
+            dealt = keep.tile([P, PACK * N], BF16, name=name + "_dealt", tag=name + "_dealt", align_bytes=64)
             dst = dealt[:].rearrange("p (h i m j) -> p h m j i", h=2, i=2, j=PACK)
-            if on_vector > 0:
-                nc.vector.tensor_copy(dst[:, :, :on_vector], src[:, :, :on_vector])
-            if on_vector < P:
-                nc.scalar.copy(dst[:, :, on_vector:], src[:, :, on_vector:])
+            groups = P // len(raw)
+            for part, tile in enumerate(raw):
+                src = tile[:].rearrange("p j (m h i) -> p h m j i", h=2, i=2)
+                m0 = part * groups
+                cut = min(P - vector_groups - m0, groups)
+                if cut < groups:
+                    nc.vector.tensor_copy(dst[:, :, m0 + cut : m0 + groups], src[:, :, cut:])
+                nc.scalar.copy(dst[:, :, m0 : m0 + cut], src[:, :, :cut])
             return dealt
 
         def quantise_weight(dealt, name, parts):
             words = keep.tile([P, N], U32, name=name + "_words", align_bytes=64)
             scales = keep.tile([P, N], U8, name=name + "_scales", align_bytes=64)
-            for h in range(parts):
-                cols = slice(h * N // parts, (h + 1) * N // parts)
-                nc.vector.quantize_mx(words[:, cols].bitcast(FP8X4), scales[:, cols], dealt[:, PACK * cols.start : PACK * cols.stop])
+            for part in range(parts):
+                cols = slice(part * N // parts, (part + 1) * N // parts)
+                values = dealt[:, PACK * cols.start : PACK * cols.stop]
+                nc.vector.quantize_mx(words[:, cols].bitcast(FP8X4), scales[:, cols], values)
             return words, scales
 
         def product(acc, weight, t, moving, cols):
@@ -126,153 +143,138 @@ def tile_picked_ymolfrg_min_po_kernel(
             )
 
         x_picked = pick(x_table, x_scale_table, offs_sb, "x_picked", "x_picked_words")
-        w1_q = quantise_weight(round_weight(w1_raw, VECTOR_CAST[0], "w1"), "w1", 2)
+        w1_q = quantise_weight(round_weight(w1_raw, VECTOR_GROUPS_W1, "w1"), "w1", 2)
         for t in range(PACK):
             bank = psum.tile([P, S], F32, name="bank")
             product(bank[:], w1_q, t, x_picked, slice(0, S))
             nc.scalar.activation(neg_y[t][:, :S], bank[:], ACT.Copy, scale=-1.0)
 
         e_picked = pick(e_table, e_scale_table, nei_sb, "e_picked", "w1_dealt")
-        w2_q = quantise_weight(round_weight(w2_raw, VECTOR_CAST[1], "w2"), "w2", 2)
+        w2_q = quantise_weight(round_weight(w2_raw, VECTOR_GROUPS_W2, "w2"), "w2", 2)
 
         starts = [sum(CHUNKS[:c]) for c in range(len(CHUNKS))]
+        last = len(CHUNKS) - 1
 
         def entries(offsets, c):
-            return offsets[:, starts[c] // 16 : (starts[c] + CHUNKS[c]) // 16]
+            return offsets[:, starts[c] // LIST_ROWS : (starts[c] + CHUNKS[c]) // LIST_ROWS]
 
         core = [keep.tile([P, PACK, n], F32, name=f"core{c}") for c, n in enumerate(CHUNKS)]
-        first = [keep.tile([P, PACK, n], F32, name=f"first{c}") if SCALAR_E1[c] else None for c, n in enumerate(CHUNKS)]
+        first = {c: keep.tile([P, PACK, CHUNKS[c]], F32, name=f"first{c}") for c in range(1, len(CHUNKS))}
 
         def fetch_core(c, t):
             nc.scalar.activation(core[c][:, t, :], neg_y[t][:].indirect(entries(c1_sb, c)), ACT.Copy)
 
         def fetch_first(c, t):
-            if t >= PACK - SCALAR_E1[c]:
-                nc.scalar.activation(first[c][:, t, :], ye[t][:].indirect(entries(n1_sb, c)), ACT.Copy)
+            nc.scalar.activation(first[c][:, t, :], ye[t][:].indirect(entries(n1_sb, c)), ACT.Copy)
 
         fetch_core(0, 0)
         for t in range(PACK):
             bank = psum.tile([P, S], F32, name="bank")
             product(bank[:], w2_q, t, e_picked, slice(0, S))
-            (nc.vector.tensor_copy if t < VECTOR_YE else nc.scalar.copy)(ye[t][:, :S], bank[:])
-            nc.scalar.activation(gain[t][:, :S], bank[:], ACT.Identity, scale=unit_sb[:, t : t + 1], bias=neg_unit[:, t : t + 1])
+            copy_ye = nc.vector.tensor_copy if t == 0 else nc.scalar.copy
+            copy_ye(ye[t][:, :S], bank[:])
+            nc.scalar.activation(
+                gain[t][:, :S], bank[:], ACT.Identity, scale=unit_sb[:, t : t + 1], bias=neg_unit[:, t : t + 1]
+            )
             if t + 1 < PACK:
                 fetch_core(0, t + 1)
-        for t in range(PACK):
-            fetch_first(0, t)
-        w3_dealt = round_weight(w3_raw, VECTOR_CAST[2], "w3")
+        w3_dealt = round_weight(w3_raw, VECTOR_GROUPS_W3, "w3")
 
         out_words = keep.tile([P, U], U32, name="out_words", align_bytes=64)
         out_scales = keep.tile([P, U], U8, name="out_scales", align_bytes=64)
         out_rows = out_0.rearrange("(p t) c -> p t c", t=PACK)
         word_rows = out_1[0].rearrange("p n t -> p (n t)").bitcast(I32)
 
-        def chunk_steps(c):
-            n = CHUNKS[c]
-            gap = keep.tile([P, PACK, n], F32, name=f"gap{c}")
-            low = keep.tile([P, PACK, n], F32, name=f"low{c}")
-            kept = keep.tile([P, PACK, n], F32, name=f"kept{c}")
+        gap = [keep.tile([P, PACK, n], F32, name=f"gap{c}") for c, n in enumerate(CHUNKS)]
+        low = [keep.tile([P, PACK, n], F32, name=f"low{c}") for c, n in enumerate(CHUNKS)]
+        kept = [keep.tile([P, PACK, n], F32, name=f"kept{c}") for c, n in enumerate(CHUNKS)]
 
-            def gap_of(t):
-                if t < PACK - SCALAR_E1[c]:
-                    nc.vector.tensor_tensor(gap[:, t, :], ye[t][:].indirect(entries(n1_sb, c)), core[c][:, t, :], ALU.add)
-                elif t % GAP_TILES[c] == 0:
-                    tiles = slice(t, t + GAP_TILES[c])
-                    nc.vector.tensor_tensor(gap[:, tiles, :], first[c][:, tiles, :], core[c][:, tiles, :], ALU.add)
+        def make_gap(c, t):
+            if c == 0:
+                window = ye[t][:].indirect(entries(n1_sb, c))
+                nc.vector.tensor_tensor(gap[c][:, t, :], window, core[c][:, t, :], ALU.add)
+            elif t % 2 == 0:
+                pair = slice(t, t + 2)
+                nc.vector.tensor_tensor(gap[c][:, pair, :], first[c][:, pair, :], core[c][:, pair, :], ALU.add)
 
-            def rest_of(t):
-                nc.vector.tensor_tensor(kept[:, t, :], gain[t][:].indirect(entries(n2_sb, c)), core[c][:, t, :], ALU.mult)
-                nc.vector.tensor_scalar(low[:, t, :], gap[:, t, :], 0.0, unit_sb[:, t : t + 1], ALU.min, ALU.mult)
+        def make_terms(c, t):
+            window = gain[t][:].indirect(entries(n2_sb, c))
+            nc.vector.tensor_tensor(kept[c][:, t, :], window, core[c][:, t, :], ALU.mult)
+            nc.vector.tensor_scalar(low[c][:, t, :], gap[c][:, t, :], 0.0, unit_sb[:, t : t + 1], ALU.min, ALU.mult)
 
-            return gap_of, rest_of, low, kept
-
-        def piece_steps(c, low, kept, p0, n, rounder):
+        def piece_steps(c, p0, n):
             name = f"{c}_{p0}"
             hid = keep.tile([P, PACK * n], BF16, name="hid" + name, align_bytes=64)
-            words = keep.tile([P, n], U32, name="hid_words" + name, align_bytes=64)
-            scales = keep.tile([P, n], U8, name="hid_scales" + name, align_bytes=64)
+            hid_words = keep.tile([P, n], U32, name="hid_words" + name, align_bytes=64)
+            hid_scales = keep.tile([P, n], U8, name="hid_scales" + name, align_bytes=64)
             result = keep.tile([P, PACK, n], F32, name="result" + name)
             rounded = keep.tile([P, PACK * n], BF16, name="rounded" + name, align_bytes=64)
             cols = slice(starts[c] + p0, starts[c] + p0 + n)
 
             def weave():
-                walk = "p t (c i) -> p c t i"
+                mine = slice(p0, p0 + n)
                 nc.vector.tensor_tensor(
-                    hid[:].rearrange("p (c i t) -> p c t i", i=2, t=PACK),
-                    kept[:, :, p0 : p0 + n].rearrange(walk, i=2),
-                    low[:, :, p0 : p0 + n].rearrange(walk, i=2),
-                    ALU.add,
+                    woven(hid[:]), row_tiles(kept[c][:, :, mine]), row_tiles(low[c][:, :, mine]), ALU.add
                 )
 
             def multiply(w3_q):
-                nc.vector.quantize_mx(words[:].bitcast(FP8X4), scales[:], hid[:])
-                for s0 in range(0, n, SUB):
-                    sub = slice(s0, s0 + SUB)
-                    if rounder == "split":
-                        for half, copy in ((0, nc.scalar.copy), (1, nc.vector.tensor_copy)):
-                            bank = psum.tile([P, 2, SUB], F32, name="bank")
-                            for t in range(2):
-                                product(bank[:, t, :], w3_q, 2 * half + t, (words, scales), sub)
-                            copy(result[:, 2 * half : 2 * half + 2, sub], bank[:])
-                        continue
-                    bank = psum.tile([P, PACK, SUB], F32, name="bank")
-                    for t in range(PACK):
-                        product(bank[:, t, :], w3_q, t, (words, scales), sub)
-                    if rounder == "scalar":
-                        nc.scalar.copy(
-                            rounded[:, PACK * s0 : PACK * (s0 + SUB)].rearrange("p (c i t) -> p c t i", i=2, t=PACK),
-                            bank[:].rearrange("p t (c i) -> p c t i", i=2),
-                        )
-                    nc.scalar.copy(result[:, :, sub], bank[:])
+                nc.vector.quantize_mx(hid_words[:].bitcast(FP8X4), hid_scales[:], hid[:])
+                hid_q = (hid_words, hid_scales)
+                if cols.stop == U:
+                    for half, copy_out in enumerate((nc.scalar.copy, nc.vector.tensor_copy)):
+                        bank = psum.tile([P, 2, n], F32, name="bank")
+                        for i in range(2):
+                            product(bank[:, i, :], w3_q, 2 * half + i, hid_q, slice(0, n))
+                        copy_out(result[:, 2 * half : 2 * half + 2, :], bank[:])
+                else:
+                    for s0 in range(0, n, BANK_COLS):
+                        part = slice(s0, s0 + BANK_COLS)
+                        bank = psum.tile([P, PACK, BANK_COLS], F32, name="bank")
+                        for t in range(PACK):
+                            product(bank[:, t, :], w3_q, t, hid_q, part)
+                        if c < last:
+                            nc.scalar.copy(woven(rounded[:, PACK * part.start : PACK * part.stop]), row_tiles(bank[:]))
+                        nc.scalar.copy(result[:, :, part], bank[:])
                 nc.sync.dma_start(out_rows[:, :, cols], result[:])
 
-            def planes():
-                if rounder != "scalar":
-                    nc.vector.tensor_copy(
-                        rounded[:].rearrange("p (c i t) -> p c t i", i=2, t=PACK),
-                        result[:].rearrange("p t (c i) -> p c t i", i=2),
-                    )
+            def make_planes():
+                if c == last:
+                    nc.vector.tensor_copy(woven(rounded[:]), row_tiles(result[:]))
                 nc.vector.quantize_mx(out_words[:, cols].bitcast(FP8X4), out_scales[:, cols], rounded[:])
-                nc.sync.dma_start(word_rows[:, cols], out_words[:, cols].bitcast(I32))
+                if cols.stop in (starts[last], U):
+                    done = slice(starts[last] if c == last else 0, cols.stop)
+                    nc.sync.dma_start(word_rows[:, done], out_words[:, done].bitcast(I32))
 
-            return weave, multiply, planes
+            return weave, multiply, make_planes
 
-        steps = chunk_steps(0)
-        steps[0](0)
-        pending = None
-        w3_q = None
-        piece = 0
-        for c in range(len(CHUNKS)):
-            gap_of, rest_of, low, kept = steps
-            more = c + 1 < len(CHUNKS)
-            if more:
+        make_gap(0, 0)
+        planes_due = []
+        for c, n in enumerate(CHUNKS):
+            if c < last:
                 for t in range(PACK):
                     fetch_core(c + 1, t)
                     fetch_first(c + 1, t)
             for t in range(PACK):
-                rest_of(t)
+                make_terms(c, t)
                 if t + 1 < PACK:
-                    gap_of(t + 1)
-            if w3_q is None:
+                    make_gap(c, t + 1)
+            if c == 0:
                 w3_q = quantise_weight(w3_dealt, "w3", 1)
-            p0 = 0
-            made = []
-            for n in PIECES[c]:
-                made.append(piece_steps(c, low, kept, p0, n, ROUNDER[piece]))
-                p0 = p0 + n
-                piece = piece + 1
-            made[0][0]()
-            for i, (weave, multiply, planes) in enumerate(made):
-                if i + 1 < len(made):
-                    made[i + 1][0]()
-                elif more:
-                    steps = chunk_steps(c + 1)
-                    steps[0](0)
+            width = BANK_COLS if c == last else n
+            pieces = [piece_steps(c, p0, width) for p0 in range(0, n, width)]
+            for weave, multiply, make_planes in pieces:
+                weave()
+            if c < last:
+                make_gap(c + 1, 0)
+            for weave, multiply, make_planes in pieces:
                 multiply(w3_q)
-                if pending is not None:
-                    pending()
-                pending = planes
-        pending()
-        for q in range(4):
+            for make_planes in planes_due:
+                make_planes()
+            planes_due = [make_planes for weave, multiply, make_planes in pieces]
+        for make_planes in planes_due:
+            make_planes()
+
+        for q in range(P // QUADRANT):
             queue = nc.sync if q % 2 == 0 else nc.scalar
-            queue.dma_start(out_2[0, 4 * q : 4 * q + 4, :].bitcast(I32), out_scales[32 * q : 32 * q + 4, :].bitcast(I32))
+            rows = out_scales[QUADRANT * q : QUADRANT * q + PACK, :]
+            queue.dma_start(out_2[0, PACK * q : PACK * (q + 1), :].bitcast(I32), rows.bitcast(I32))

from contextlib import ExitStack

import concourse.mybir as mybir

K, T, S, N, U = 512, 1024, 512, 512, 1024
FLOPS = 2 * (2 * K * N * S) + 2 * N * N * U

F32 = mybir.dt.float32
BF16 = mybir.dt.bfloat16
I32 = mybir.dt.int32
U32 = mybir.dt.uint32
U16 = mybir.dt.uint16
U8 = mybir.dt.uint8
FP8X4 = mybir.dt.float8_e4m3fn_x4
ALU = mybir.AluOpType
ACT = mybir.ActivationFunctionType

P = 128
PACK = 4
QUADRANT = 32
LIST_ROWS = 16
BANKS = 8
SPARE = 16
BANK_COLS = 128
CHUNKS = (512, 256, 256)
VECTOR_GROUPS_W1, VECTOR_GROUPS_W2, VECTOR_GROUPS_W3 = 52, 96, 0
WOVEN = "p (c i t) -> p c t i"
ROW_TILES = "p t (c i) -> p c t i"


def woven(ap):
    return ap.rearrange(WOVEN, i=2, t=PACK)


def row_tiles(ap):
    return ap.rearrange(ROW_TILES, i=2)


def tile_picked_ymolfrg_min_po_kernel(
    tc, x_words, x_scales, w1, e_words, e_scales, w2, unit, w3, offs, nei, c1, n1, n2, out_0, out_1, out_2
):
    nc = tc.nc
    with ExitStack() as ctx:
        keep = ctx.enter_context(tc.tile_pool(name="keep", bufs=1))
        psum = ctx.enter_context(tc.psum_pool(name="psum", bufs=BANKS))

        def load_list(src, name):
            tile = keep.tile(list(src.shape), U16, name=name)
            nc.sync.dma_start(tile[:], src)
            return tile

        def load_words(src, name):
            tile = keep.tile([P, T], I32, name=name)
            nc.sync.dma_start(tile[:], src[0].rearrange("p n t -> p (n t)").bitcast(I32))
            return tile

        def load_scales(src, name):
            tile = keep.tile([P, T], U8, name=name)
            nc.vector.memset(tile[:].bitcast(I32), 0)
            for q in range(P // QUADRANT):
                rows = tile[QUADRANT * q : QUADRANT * q + PACK, :]
                nc.sync.dma_start(rows.bitcast(I32), src[0, PACK * q : PACK * (q + 1), :].bitcast(I32))
            return tile

        def load_weight(src, name, parts):
            tiles = []
            for part in range(parts):
                tile = keep.tile([P, PACK, N // parts], F32, name=f"{name}{part}")
                cols = slice(part * N // parts, (part + 1) * N // parts)
                nc.sync.dma_start(tile[:], src.rearrange("(p j) c -> p j c", j=PACK)[:, :, cols])
                tiles.append(tile)
            return tiles

        offs_sb = load_list(offs, "offs_sb")
        x_table = load_words(x_words, "x_table")
        x_scale_table = load_scales(x_scales, "x_scale_table")
        w1_raw = load_weight(w1, "w1_raw", 2)
        e_table = load_words(e_words, "e_table")
        nei_sb = load_list(nei, "nei_sb")
        e_scale_table = load_scales(e_scales, "e_scale_table")
        w2_raw = load_weight(w2, "w2_raw", 1)
        c1_sb = load_list(c1, "c1_sb")
        unit_sb = keep.tile([P, PACK], F32, name="unit_sb")
        nc.sync.dma_start(unit_sb[:], unit.rearrange("(p t) o -> p (t o)", t=PACK))
        n1_sb = load_list(n1, "n1_sb")
        n2_sb = load_list(n2, "n2_sb")
        w3_raw = load_weight(w3, "w3_raw", 1)

        def windows(name):
            tiles = []
            for t in range(PACK):
                tile = keep.tile([P, S + SPARE], F32, name=f"{name}{t}")
                nc.vector.memset(tile[:, S:], 0.0)
                tiles.append(tile)
            return tiles

        neg_y = windows("neg_y")
        ye = windows("ye")
        gain = windows("gain")

        neg_unit = keep.tile([P, PACK], F32, name="neg_unit")
        nc.scalar.activation(neg_unit[:], unit_sb[:], ACT.Copy, scale=-1.0)

        def pick(table, scale_table, offsets, name, tag):
            words = keep.tile([P, S], U32, name=name + "_words", tag=tag, align_bytes=64)
            scales = keep.tile([P, S], U8, name=name + "_scales", align_bytes=64)
            nc.vector.tensor_copy(words[:], table[:].bitcast(U32).indirect(offsets[:]))
            nc.vector.tensor_copy(scales[:], scale_table[:].indirect(offsets[:]))
            return words, scales

        def round_weight(raw, vector_groups, name):
            dealt = keep.tile([P, PACK * N], BF16, name=name + "_dealt", tag=name + "_dealt", align_bytes=64)
            dst = dealt[:].rearrange("p (h i m j) -> p h m j i", h=2, i=2, j=PACK)
            groups = P // len(raw)
            for part, tile in enumerate(raw):
                src = tile[:].rearrange("p j (m h i) -> p h m j i", h=2, i=2)
                m0 = part * groups
                cut = min(P - vector_groups - m0, groups)
                if cut < groups:
                    nc.vector.tensor_copy(dst[:, :, m0 + cut : m0 + groups], src[:, :, cut:])
                nc.scalar.copy(dst[:, :, m0 : m0 + cut], src[:, :, :cut])
            return dealt

        def quantise_weight(dealt, name, parts):
            words = keep.tile([P, N], U32, name=name + "_words", align_bytes=64)
            scales = keep.tile([P, N], U8, name=name + "_scales", align_bytes=64)
            for part in range(parts):
                cols = slice(part * N // parts, (part + 1) * N // parts)
                values = dealt[:, PACK * cols.start : PACK * cols.stop]
                nc.vector.quantize_mx(words[:, cols].bitcast(FP8X4), scales[:, cols], values)
            return words, scales

        def product(acc, weight, t, moving, cols):
            rows = slice(t * P, (t + 1) * P)
            nc.tensor.matmul_mx(
                out=acc,
                lhsT=weight[0][:, rows].bitcast(FP8X4),
                lhsT_scale=weight[1][:, rows],
                rhs=moving[0][:, cols].bitcast(FP8X4),
                rhs_scale=moving[1][:, cols],
                start=True,
                stop=True,
            )

        x_picked = pick(x_table, x_scale_table, offs_sb, "x_picked", "x_picked_words")
        w1_q = quantise_weight(round_weight(w1_raw, VECTOR_GROUPS_W1, "w1"), "w1", 2)
        for t in range(PACK):
            bank = psum.tile([P, S], F32, name="bank")
            product(bank[:], w1_q, t, x_picked, slice(0, S))
            nc.scalar.activation(neg_y[t][:, :S], bank[:], ACT.Copy, scale=-1.0)

        e_picked = pick(e_table, e_scale_table, nei_sb, "e_picked", "w1_dealt")
        w2_q = quantise_weight(round_weight(w2_raw, VECTOR_GROUPS_W2, "w2"), "w2", 2)

        starts = [sum(CHUNKS[:c]) for c in range(len(CHUNKS))]
        last = len(CHUNKS) - 1

        def entries(offsets, c):
            return offsets[:, starts[c] // LIST_ROWS : (starts[c] + CHUNKS[c]) // LIST_ROWS]

        core = [keep.tile([P, PACK, n], F32, name=f"core{c}") for c, n in enumerate(CHUNKS)]
        first = {c: keep.tile([P, PACK, CHUNKS[c]], F32, name=f"first{c}") for c in range(1, len(CHUNKS))}

        def fetch_core(c, t):
            nc.scalar.activation(core[c][:, t, :], neg_y[t][:].indirect(entries(c1_sb, c)), ACT.Copy)

        def fetch_first(c, t):
            nc.scalar.activation(first[c][:, t, :], ye[t][:].indirect(entries(n1_sb, c)), ACT.Copy)

        fetch_core(0, 0)
        for t in range(PACK):
            bank = psum.tile([P, S], F32, name="bank")
            product(bank[:], w2_q, t, e_picked, slice(0, S))
            copy_ye = nc.vector.tensor_copy if t == 0 else nc.scalar.copy
            copy_ye(ye[t][:, :S], bank[:])
            nc.scalar.activation(
                gain[t][:, :S], bank[:], ACT.Identity, scale=unit_sb[:, t : t + 1], bias=neg_unit[:, t : t + 1]
            )
            if t + 1 < PACK:
                fetch_core(0, t + 1)
        w3_dealt = round_weight(w3_raw, VECTOR_GROUPS_W3, "w3")

        out_words = keep.tile([P, U], U32, name="out_words", align_bytes=64)
        out_scales = keep.tile([P, U], U8, name="out_scales", align_bytes=64)
        out_rows = out_0.rearrange("(p t) c -> p t c", t=PACK)
        word_rows = out_1[0].rearrange("p n t -> p (n t)").bitcast(I32)

        gap = [keep.tile([P, PACK, n], F32, name=f"gap{c}") for c, n in enumerate(CHUNKS)]
        low = [keep.tile([P, PACK, n], F32, name=f"low{c}") for c, n in enumerate(CHUNKS)]
        kept = [keep.tile([P, PACK, n], F32, name=f"kept{c}") for c, n in enumerate(CHUNKS)]

        def make_gap(c, t):
            if c == 0:
                window = ye[t][:].indirect(entries(n1_sb, c))
                nc.vector.tensor_tensor(gap[c][:, t, :], window, core[c][:, t, :], ALU.add)
            elif t % 2 == 0:
                pair = slice(t, t + 2)
                nc.vector.tensor_tensor(gap[c][:, pair, :], first[c][:, pair, :], core[c][:, pair, :], ALU.add)

        def make_terms(c, t):
            window = gain[t][:].indirect(entries(n2_sb, c))
            nc.vector.tensor_tensor(kept[c][:, t, :], window, core[c][:, t, :], ALU.mult)
            nc.vector.tensor_scalar(low[c][:, t, :], gap[c][:, t, :], 0.0, unit_sb[:, t : t + 1], ALU.min, ALU.mult)

        def piece_steps(c, p0, n):
            name = f"{c}_{p0}"
            hid = keep.tile([P, PACK * n], BF16, name="hid" + name, align_bytes=64)
            hid_words = keep.tile([P, n], U32, name="hid_words" + name, align_bytes=64)
            hid_scales = keep.tile([P, n], U8, name="hid_scales" + name, align_bytes=64)
            result = keep.tile([P, PACK, n], F32, name="result" + name)
            rounded = keep.tile([P, PACK * n], BF16, name="rounded" + name, align_bytes=64)
            cols = slice(starts[c] + p0, starts[c] + p0 + n)

            def weave():
                mine = slice(p0, p0 + n)
                nc.vector.tensor_tensor(
                    woven(hid[:]), row_tiles(kept[c][:, :, mine]), row_tiles(low[c][:, :, mine]), ALU.add
                )

            def multiply(w3_q):
                nc.vector.quantize_mx(hid_words[:].bitcast(FP8X4), hid_scales[:], hid[:])
                hid_q = (hid_words, hid_scales)
                if cols.stop == U:
                    for half, copy_out in enumerate((nc.scalar.copy, nc.vector.tensor_copy)):
                        bank = psum.tile([P, 2, n], F32, name="bank")
                        for i in range(2):
                            product(bank[:, i, :], w3_q, 2 * half + i, hid_q, slice(0, n))
                        copy_out(result[:, 2 * half : 2 * half + 2, :], bank[:])
                else:
                    for s0 in range(0, n, BANK_COLS):
                        part = slice(s0, s0 + BANK_COLS)
                        bank = psum.tile([P, PACK, BANK_COLS], F32, name="bank")
                        for t in range(PACK):
                            product(bank[:, t, :], w3_q, t, hid_q, part)
                        if c < last:
                            nc.scalar.copy(woven(rounded[:, PACK * part.start : PACK * part.stop]), row_tiles(bank[:]))
                        nc.scalar.copy(result[:, :, part], bank[:])
                nc.sync.dma_start(out_rows[:, :, cols], result[:])

            def make_planes():
                if c == last:
                    nc.vector.tensor_copy(woven(rounded[:]), row_tiles(result[:]))
                nc.vector.quantize_mx(out_words[:, cols].bitcast(FP8X4), out_scales[:, cols], rounded[:])
                if cols.stop in (starts[last], U):
                    done = slice(starts[last] if c == last else 0, cols.stop)
                    nc.sync.dma_start(word_rows[:, done], out_words[:, done].bitcast(I32))

            return weave, multiply, make_planes

        make_gap(0, 0)
        planes_due = []
        for c, n in enumerate(CHUNKS):
            if c < last:
                for t in range(PACK):
                    fetch_core(c + 1, t)
                    fetch_first(c + 1, t)
            for t in range(PACK):
                make_terms(c, t)
                if t + 1 < PACK:
                    make_gap(c, t + 1)
            if c == 0:
                w3_q = quantise_weight(w3_dealt, "w3", 1)
            width = BANK_COLS if c == last else n
            pieces = [piece_steps(c, p0, width) for p0 in range(0, n, width)]
            for weave, multiply, make_planes in pieces:
                weave()
            if c < last:
                make_gap(c + 1, 0)
            for weave, multiply, make_planes in pieces:
                multiply(w3_q)
            for make_planes in planes_due:
                make_planes()
            planes_due = [make_planes for weave, multiply, make_planes in pieces]
        for make_planes in planes_due:
            make_planes()

        for q in range(P // QUADRANT):
            queue = nc.sync if q % 2 == 0 else nc.scalar
            rows = out_scales[QUADRANT * q : QUADRANT * q + PACK, :]
            queue.dma_start(out_2[0, PACK * q : PACK * (q + 1), :].bitcast(I32), rows.bitcast(I32))
